import numpy as np
import ml_dtypes


def mxq(x, axis, fmt="e4m3"):
    dtype, down = {"e4m3": (ml_dtypes.float8_e4m3fn, 7), "e5m2": (ml_dtypes.float8_e5m2, 14)}[fmt]
    v = np.moveaxis(np.asarray(x, np.float32).astype(ml_dtypes.bfloat16).astype(np.float64), axis, -1)
    blocks = v.reshape(v.shape[:-1] + (-1, 32))
    amax = np.abs(blocks).max(-1, keepdims=True)
    byte = np.maximum(np.where(amax > 0, np.frexp(amax)[1] - 1 + 127, 0) - down, 1)
    scale = np.exp2(byte - 127.0)
    codes = (blocks / scale).astype(np.float32).astype(dtype).astype(np.float64)
    return np.moveaxis((codes * scale).reshape(v.shape), -1, axis)


WIDE = False


def mx_kscale(k):
    if not WIDE:
        return np.ones(k)
    levels = np.array([10, -10, 5, -5, 0])
    if k % 512:
        return np.exp2(np.random.permutation(np.resize(levels, k // 32))).repeat(32)
    a = np.empty((k // 512, 16))
    for p in range(k // 512):
        a[p, :8] = np.random.permutation(np.resize(levels, 8))
        for g in range(8):
            far = levels[np.abs(levels - a[p, g]) >= 10]
            a[p, g + 8] = far[np.random.randint(len(far))]
    return np.exp2(a.ravel()).repeat(32)


def f64(x):
    return np.asarray(x).astype(np.float64)


def striped(idx):
    return np.tile(idx.reshape(-1, 16).T, (8, 1)).astype(np.uint16)


def unstriped(offs):
    return offs[:16].T.reshape(-1).astype(np.int64)


def pack_weight(w):
    k, n = w.shape
    w = f64(np.asarray(w, np.float32).astype(ml_dtypes.bfloat16)).reshape(k // 32, 32, n)
    amax = np.abs(w).max(1)
    byte = np.clip(np.where(amax > 0, np.frexp(amax)[1] - 1 + 127 - 7, 1), 1, 254)
    scaled = (w * np.exp2(127.0 - byte)[:, None, :]).reshape(k, n).astype(np.float32)
    words = np.ascontiguousarray(scaled.reshape(k // 512, 128, 4, n).transpose(0, 1, 3, 2)).astype(ml_dtypes.float8_e4m3fn).view(np.uint8)
    return words, np.ascontiguousarray(byte.astype(np.uint8).reshape(k // 512, 16, n))


def unpack_weight(words, scales):
    g, p, n, _ = words.shape
    vals = np.ascontiguousarray(words).view(ml_dtypes.float8_e4m3fn).astype(np.float64) * np.repeat(np.exp2(scales.astype(np.float64) - 127.0), 8, axis=1)[..., None]
    return vals.transpose(0, 1, 3, 2).reshape(g * 512, n)


def relu(v):
    return np.maximum(v, 0.0)


K, T, E, C, N = 1536, 512, 4, 256, 512


def by_expert(wq, xq):
    return np.concatenate([wq[e].T @ xq[:, e * C:(e + 1) * C] for e in range(E)], axis=1)


def setup_inputs():
    n = np.random.standard_normal
    s = mx_kscale(K)[:, None]
    first = np.random.permutation(np.repeat(np.arange(E), T // E))
    second = (first + 1 + np.random.permutation(np.repeat(np.arange(E - 1), -(-T // (E - 1)))[:T])) % E
    while np.bincount(second, minlength=E).max() != T // E:
        load = np.bincount(second, minlength=E); hi, lo = int(load.argmax()), int(load.argmin())
        t = np.flatnonzero((second == hi) & (first != lo))[0]; second[t] = lo
    slot_token = np.empty(E * C, np.int64); pos = np.empty((2, T), np.int64); fill = np.zeros(E, np.int64)
    place = np.stack([np.random.permutation(C) for _ in range(E)])
    for r, deal in enumerate((first, second)):
        for t in np.random.permutation(T):
            e = deal[t]; j = e * C + place[e, fill[e]]; fill[e] += 1; slot_token[j] = t; pos[r, t] = j
    g = np.random.uniform(0.2, 0.8, T)
    packed = [pack_weight(m) for m in n((E, K, N)) / np.sqrt(K) / s[None]]
    return {
        "xT": (n((K, T)) * s).astype(np.float32),
        "w_words": np.stack([m[0] for m in packed]),
        "w_scales": np.stack([m[1] for m in packed]),
        "b": (0.3 * n((N, E))).astype(np.float32),
        "gate": np.stack([np.tile(g, (N, 1)), np.tile(1.0 - g, (N, 1))]).astype(np.float32),
        "offs": striped(slot_token),
        "pos1": striped(pos[0]),
        "pos2": striped(pos[1]),
    }


def reference(xT, w_words, w_scales, b, gate, offs, pos1, pos2):
    idx = unstriped(offs)
    xq = mxq(f64(xT)[:, idx], 0, "e4m3")
    w = np.stack([unpack_weight(w_words[e], w_scales[e]) for e in range(E)])
    y = by_expert(w, xq)
    y = relu(y + np.repeat(f64(b), C, axis=1))
    return f64(gate[0]) * y[:, unstriped(pos1)] + f64(gate[1]) * y[:, unstriped(pos2)]

@@ -1,0 +1,163 @@
+from contextlib import ExitStack
+
+import concourse.mybir as mybir
+
+K, T, E, C, N = 1536, 512, 4, 256, 512
+P = 128
+PACK = 4
+PASSES = K // (P * PACK)
+BLOCKS = N // P
+SLOTS = E * C
+FLOPS = 2 * K * SLOTS * N
+
+F32 = mybir.dt.float32
+BF16 = mybir.dt.bfloat16
+I32 = mybir.dt.int32
+U32 = mybir.dt.uint32
+U16 = mybir.dt.uint16
+U8 = mybir.dt.uint8
+FP8X4 = mybir.dt.float8_e4m3fn_x4
+MULT = mybir.AluOpType.mult
+ADD = mybir.AluOpType.add
+RELU = mybir.ActivationFunctionType.Relu
+
+HALF = T // 2
+HALF_N = N // 2
+
+
+def tile_routed_moe_kernel(tc, xT, w_words, w_scales, b, gate, offs, pos1, pos2, out):
+    nc = tc.nc
+    with ExitStack() as ctx:
+        keep = ctx.enter_context(tc.tile_pool(name="keep", bufs=1))
+        psum = ctx.enter_context(tc.psum_pool(name="psum", bufs=1))
+
+        offs_t = keep.tile([P, SLOTS // 16], U16, name="offs_t")
+        pos1_t = keep.tile([P, T // 16], U16, name="pos1_t")
+        pos2_t = keep.tile([P, T // 16], U16, name="pos2_t")
+
+        raw = [[keep.tile([P, PACK, HALF], F32, name=f"raw{a}_{h}") for h in range(2)] for a in range(PASSES)]
+        xb = [keep.tile([P, T, PACK], BF16, name=f"xb{a}", align_bytes=64) for a in range(PASSES)]
+        xw = [keep.tile([P, T], U32, name=f"xw{a}", align_bytes=64) for a in range(PASSES)]
+        xs = keep.tile([P, T], U8, name="xs", align_bytes=64)
+        gw = [keep.tile([P, SLOTS], U32, name=f"gw{a}", align_bytes=64) for a in range(PASSES)]
+        gs = keep.tile([P, SLOTS], U8, name="gs", align_bytes=64)
+        ww = [keep.tile([P, E * PASSES, HALF_N], U32, name=f"ww{h}", align_bytes=64) for h in range(2)]
+        ws = keep.tile([P, E, N], U8, name="ws", align_bytes=64)
+        bias = keep.tile([P, BLOCKS, E], F32, name="bias")
+        gt = [keep.tile([P, 2, T], F32, name=f"gt{m}") for m in range(BLOCKS)]
+        y = [keep.tile([P, SLOTS], F32, name=f"y{m}") for m in range(BLOCKS)]
+        t1 = [keep.tile([P, T], F32, name=f"t1_{m}") for m in range(BLOCKS)]
+        t2 = [keep.tile([P, T], F32, name=f"t2_{m}") for m in range(BLOCKS)]
+        res = [keep.tile([P, T], F32, name=f"res{m}") for m in range(BLOCKS)]
+        acc = [[psum.tile([P, 2 * C], F32, name=f"acc{m}_{h}") for h in range(2)] for m in range(BLOCKS)]
+
+        nc.gpsimd.memset(xs[:], 0)
+        nc.gpsimd.memset(ws[:].rearrange("p e n -> p (e n)").bitcast(I32), 0)
+
+        def load_x(a, h):
+            src = xT[a * P * PACK : (a + 1) * P * PACK, h * HALF : (h + 1) * HALF]
+            nc.sync.dma_start(raw[a][h][:], src.rearrange("(p j) t -> p j t", j=PACK))
+
+        def load_w(h):
+            src = w_words[:, :, :, h * HALF_N : (h + 1) * HALF_N, :].rearrange("e a p n r -> p (e a) (n r)")
+            nc.sync.dma_start(ww[h][:].bitcast(I32), src.bitcast(I32))
+
+        load_x(0, 0)
+        load_x(0, 1)
+        nc.sync.dma_start(offs_t[:], offs)
+        for a in range(1, PASSES):
+            for h in range(2):
+                load_x(a, h)
+        nc.scalar.dma_start(bias[:], b.rearrange("(m p) e -> p m e", p=P))
+        for a in range(PASSES):
+            for q in range(4):
+                rows = slice(32 * q + 4 * a, 32 * q + 4 * a + 4)
+                nc.sync.dma_start(
+                    ws[rows, :, :].bitcast(I32),
+                    w_scales[:, a, 4 * q : 4 * q + 4, :].rearrange("e q n -> q e n").bitcast(I32),
+                )
+        def load_gate(m):
+            nc.sync.dma_start(gt[m][:], gate[:, m * P : (m + 1) * P, :].rearrange("r p t -> p r t"))
+
+        load_w(0)
+        nc.sync.dma_start(pos1_t[:], pos1)
+        nc.sync.dma_start(pos2_t[:], pos2)
+        load_gate(0)
+        load_w(1)
+        for m in range(1, BLOCKS):
+            load_gate(m)
+
+        def interleave(copy, a, h):
+            dst = xb[a][:, h * HALF : (h + 1) * HALF, :].rearrange("p (c i) j -> p c j i", i=4)
+            copy(dst, raw[a][h][:].rearrange("p j (c i) -> p c j i", i=4))
+
+        def quantize(a, t0, t1_):
+            nc.vector.quantize_mx(
+                out=xw[a][:, t0:t1_].bitcast(FP8X4),
+                scales=xs[4 * a : P, t0:t1_],
+                in_=xb[a][:, t0:t1_, :].rearrange("p t j -> p (t j)"),
+            )
+
+        def gather_words(a, s0, s1):
+            nc.vector.tensor_copy(gw[a][:, s0:s1], xw[a][:].indirect(offs_t[:, s0 // 16 : s1 // 16]))
+
+        def gather_scales(s0, s1):
+            nc.vector.tensor_copy(gs[:, s0:s1], xs[:].indirect(offs_t[:, s0 // 16 : s1 // 16]))
+
+        def multiply(m, e):
+            for a in range(PASSES):
+                nc.tensor.matmul_mx(
+                    out=acc[m][e // 2][:, (e % 2) * C : (e % 2 + 1) * C],
+                    lhsT=ww[m // 2][:, e * PASSES + a, (m % 2) * P : (m % 2 + 1) * P].bitcast(FP8X4),
+                    lhsT_scale=ws[4 * a : P, e, m * P : (m + 1) * P],
+                    rhs=gw[a][:, e * C : (e + 1) * C].bitcast(FP8X4),
+                    rhs_scale=gs[4 * a : P, e * C : (e + 1) * C],
+                    start=(a == 0),
+                    stop=(a == PASSES - 1),
+                )
+
+        def empty(m, e):
+            nc.scalar.activation(
+                y[m][:, e * C : (e + 1) * C], acc[m][e // 2][:, (e % 2) * C : (e % 2 + 1) * C], RELU, bias=bias[:, m, e : e + 1]
+            )
+
+        interleave(nc.scalar.copy, 0, 0)
+        interleave(nc.vector.tensor_copy, 0, 1)
+        quantize(0, 0, HALF)
+        quantize(0, HALF, T)
+        for s0, s1 in ((0, 384), (384, 768), (768, 1024)):
+            gather_words(0, s0, s1)
+        interleave(nc.scalar.copy, 1, 0)
+        interleave(nc.scalar.copy, 1, 1)
+        quantize(1, 0, T)
+        for s0, s1 in ((0, 384), (384, 768), (768, 1024)):
+            gather_words(1, s0, s1)
+        interleave(nc.scalar.copy, 2, 0)
+        interleave(nc.scalar.copy, 2, 1)
+        quantize(2, 0, T)
+        for e in range(E):
+            gather_scales(e * C, (e + 1) * C)
+            gather_words(2, e * C, (e + 1) * C)
+            multiply(0, e)
+            empty(0, e)
+        for m in range(1, BLOCKS):
+            for e in range(E):
+                multiply(m, e)
+                empty(m, e)
+
+        def first(m):
+            nc.vector.tensor_tensor(t1[m][:], y[m][:].indirect(pos1_t[:]), gt[m][:, 0, :], MULT)
+
+        def second(m):
+            nc.vector.tensor_tensor(t2[m][:], y[m][:].indirect(pos2_t[:]), gt[m][:, 1, :], MULT)
+
+        def finish(m):
+            nc.vector.tensor_tensor(res[m][:], t1[m][:], t2[m][:], ADD)
+            nc.sync.dma_start(out[m * P : (m + 1) * P, :], res[m][:])
+
+        for m in range(BLOCKS):
+            first(m)
+            if m > 0:
+                finish(m - 1)
+            second(m)
+        finish(BLOCKS - 1)

@@ -21,9 +21,6 @@ MULT = mybir.AluOpType.mult
 ADD = mybir.AluOpType.add
 RELU = mybir.ActivationFunctionType.Relu
 
-HALF = T // 2
-HALF_N = N // 2
-
 
 def tile_routed_moe_kernel(tc, xT, w_words, w_scales, b, gate, offs, pos1, pos2, out):
     nc = tc.nc
@@ -34,68 +31,70 @@ def tile_routed_moe_kernel(tc, xT, w_words, w_scales, b, gate, offs, pos1, pos2,
         offs_t = keep.tile([P, SLOTS // 16], U16, name="offs_t")
         pos1_t = keep.tile([P, T // 16], U16, name="pos1_t")
         pos2_t = keep.tile([P, T // 16], U16, name="pos2_t")
-
-        raw = [[keep.tile([P, PACK, HALF], F32, name=f"raw{a}_{h}") for h in range(2)] for a in range(PASSES)]
+        raw = [keep.tile([P, PACK, T], F32, name=f"raw{a}") for a in range(PASSES)]
         xb = [keep.tile([P, T, PACK], BF16, name=f"xb{a}", align_bytes=64) for a in range(PASSES)]
         xw = [keep.tile([P, T], U32, name=f"xw{a}", align_bytes=64) for a in range(PASSES)]
         xs = keep.tile([P, T], U8, name="xs", align_bytes=64)
         gw = [keep.tile([P, SLOTS], U32, name=f"gw{a}", align_bytes=64) for a in range(PASSES)]
         gs = keep.tile([P, SLOTS], U8, name="gs", align_bytes=64)
-        ww = [keep.tile([P, E * PASSES, HALF_N], U32, name=f"ww{h}", align_bytes=64) for h in range(2)]
+        ww = [keep.tile([P, PASSES, N], U32, name=f"ww{e}", align_bytes=64) for e in range(E)]
         ws = keep.tile([P, E, N], U8, name="ws", align_bytes=64)
         bias = keep.tile([P, BLOCKS, E], F32, name="bias")
         gt = [keep.tile([P, 2, T], F32, name=f"gt{m}") for m in range(BLOCKS)]
         y = [keep.tile([P, SLOTS], F32, name=f"y{m}") for m in range(BLOCKS)]
-        t1 = [keep.tile([P, T], F32, name=f"t1_{m}") for m in range(BLOCKS)]
-        t2 = [keep.tile([P, T], F32, name=f"t2_{m}") for m in range(BLOCKS)]
-        res = [keep.tile([P, T], F32, name=f"res{m}") for m in range(BLOCKS)]
-        acc = [[psum.tile([P, 2 * C], F32, name=f"acc{m}_{h}") for h in range(2)] for m in range(BLOCKS)]
 
         nc.gpsimd.memset(xs[:], 0)
         nc.gpsimd.memset(ws[:].rearrange("p e n -> p (e n)").bitcast(I32), 0)
 
-        def load_x(a, h):
-            src = xT[a * P * PACK : (a + 1) * P * PACK, h * HALF : (h + 1) * HALF]
-            nc.sync.dma_start(raw[a][h][:], src.rearrange("(p j) t -> p j t", j=PACK))
+        def load_x(a):
+            src = xT[a * P * PACK : (a + 1) * P * PACK, :]
+            nc.sync.dma_start(raw[a][:], src.rearrange("(p j) t -> p j t", j=PACK))
 
-        def load_w(h):
-            src = w_words[:, :, :, h * HALF_N : (h + 1) * HALF_N, :].rearrange("e a p n r -> p (e a) (n r)")
-            nc.sync.dma_start(ww[h][:].bitcast(I32), src.bitcast(I32))
+        def load_ws(i):
+            a, q = i // 4, i % 4
+            rows = slice(32 * q + 4 * a, 32 * q + 4 * a + 4)
+            nc.sync.dma_start(
+                ws[rows, :, :].bitcast(I32), w_scales[:, a, 4 * q : 4 * q + 4, :].rearrange("e q n -> q e n").bitcast(I32)
+            )
 
-        load_x(0, 0)
-        load_x(0, 1)
-        nc.sync.dma_start(offs_t[:], offs)
-        for a in range(1, PASSES):
-            for h in range(2):
-                load_x(a, h)
-        nc.scalar.dma_start(bias[:], b.rearrange("(m p) e -> p m e", p=P))
-        for a in range(PASSES):
-            for q in range(4):
-                rows = slice(32 * q + 4 * a, 32 * q + 4 * a + 4)
-                nc.sync.dma_start(
-                    ws[rows, :, :].bitcast(I32),
-                    w_scales[:, a, 4 * q : 4 * q + 4, :].rearrange("e q n -> q e n").bitcast(I32),
-                )
+        def load_w(e):
+            nc.sync.dma_start(ww[e][:].bitcast(I32), w_words[e].rearrange("a p n r -> p a (n r)").bitcast(I32))
+
         def load_gate(m):
             nc.sync.dma_start(gt[m][:], gate[:, m * P : (m + 1) * P, :].rearrange("r p t -> p r t"))
 
+        def load_bias():
+            nc.sync.dma_start(bias[:], b.rearrange("(m p) e -> p m e", p=P))
+
+        def load_pos():
+            nc.sync.dma_start(pos1_t[:], pos1)
+            nc.sync.dma_start(pos2_t[:], pos2)
+
+        load_x(0)
+        nc.sync.dma_start(offs_t[:], offs)
+        for i in range(0, 4):
+            load_ws(i)
+        load_x(1)
+        load_x(2)
+        for i in range(4, 10):
+            load_ws(i)
         load_w(0)
-        nc.sync.dma_start(pos1_t[:], pos1)
-        nc.sync.dma_start(pos2_t[:], pos2)
-        load_gate(0)
-        load_w(1)
-        for m in range(1, BLOCKS):
+        for i in range(10, 12):
+            load_ws(i)
+        load_bias()
+        for e in range(1, E):
+            load_w(e)
+        load_pos()
+        for m in range(BLOCKS):
             load_gate(m)
 
-        def interleave(copy, a, h):
-            dst = xb[a][:, h * HALF : (h + 1) * HALF, :].rearrange("p (c i) j -> p c j i", i=4)
-            copy(dst, raw[a][h][:].rearrange("p j (c i) -> p c j i", i=4))
+        def interleave(copy, a, t0, t1):
+            dst = xb[a][:, t0:t1, :].rearrange("p (c i) j -> p c j i", i=4)
+            copy(dst, raw[a][:, :, t0:t1].rearrange("p j (c i) -> p c j i", i=4))
 
-        def quantize(a, t0, t1_):
+        def quantize(a):
             nc.vector.quantize_mx(
-                out=xw[a][:, t0:t1_].bitcast(FP8X4),
-                scales=xs[4 * a : P, t0:t1_],
-                in_=xb[a][:, t0:t1_, :].rearrange("p t j -> p (t j)"),
+                out=xw[a][:].bitcast(FP8X4), scales=xs[4 * a : P, :], in_=xb[a][:].rearrange("p t j -> p (t j)")
             )
 
         def gather_words(a, s0, s1):
@@ -104,60 +103,68 @@ def tile_routed_moe_kernel(tc, xT, w_words, w_scales, b, gate, offs, pos1, pos2,
         def gather_scales(s0, s1):
             nc.vector.tensor_copy(gs[:, s0:s1], xs[:].indirect(offs_t[:, s0 // 16 : s1 // 16]))
 
-        def multiply(m, e):
+        def multiply(acc, m, e):
             for a in range(PASSES):
                 nc.tensor.matmul_mx(
-                    out=acc[m][e // 2][:, (e % 2) * C : (e % 2 + 1) * C],
-                    lhsT=ww[m // 2][:, e * PASSES + a, (m % 2) * P : (m % 2 + 1) * P].bitcast(FP8X4),
+                    out=acc[:, e, 0:C],
+                    lhsT=ww[e][:, a, m * P : (m + 1) * P].bitcast(FP8X4),
                     lhsT_scale=ws[4 * a : P, e, m * P : (m + 1) * P],
                     rhs=gw[a][:, e * C : (e + 1) * C].bitcast(FP8X4),
                     rhs_scale=gs[4 * a : P, e * C : (e + 1) * C],
                     start=(a == 0),
                     stop=(a == PASSES - 1),
                 )
+            nc.scalar.activation(y[m][:, e * C : (e + 1) * C], acc[:, e, 0:C], RELU, bias=bias[:, m, e : e + 1])
 
-        def empty(m, e):
-            nc.scalar.activation(
-                y[m][:, e * C : (e + 1) * C], acc[m][e // 2][:, (e % 2) * C : (e % 2 + 1) * C], RELU, bias=bias[:, m, e : e + 1]
-            )
-
-        interleave(nc.scalar.copy, 0, 0)
-        interleave(nc.vector.tensor_copy, 0, 1)
-        quantize(0, 0, HALF)
-        quantize(0, HALF, T)
-        for s0, s1 in ((0, 384), (384, 768), (768, 1024)):
-            gather_words(0, s0, s1)
-        interleave(nc.scalar.copy, 1, 0)
-        interleave(nc.scalar.copy, 1, 1)
-        quantize(1, 0, T)
-        for s0, s1 in ((0, 384), (384, 768), (768, 1024)):
-            gather_words(1, s0, s1)
-        interleave(nc.scalar.copy, 2, 0)
-        interleave(nc.scalar.copy, 2, 1)
-        quantize(2, 0, T)
+        interleave(nc.scalar.copy, 0, 0, 192)
+        interleave(nc.vector.tensor_copy, 0, 192, T)
+        quantize(0)
+        interleave(nc.scalar.copy, 1, 0, 384)
+        gather_words(0, 0, 384)
+        interleave(nc.vector.tensor_copy, 1, 384, T)
+        gather_words(0, 384, 768)
+        quantize(1)
+        gather_words(0, 768, 1024)
+        interleave(nc.scalar.copy, 2, 0, 256)
+        interleave(nc.scalar.copy, 2, 256, T)
+        gather_words(1, 0, 384)
+        gather_words(1, 384, 768)
+        quantize(2)
+        gather_words(1, 768, 1024)
+        acc = psum.tile([P, 2 * E, 2 * C], F32, name="acc")
         for e in range(E):
             gather_scales(e * C, (e + 1) * C)
             gather_words(2, e * C, (e + 1) * C)
-            multiply(0, e)
-            empty(0, e)
-        for m in range(1, BLOCKS):
+            multiply(acc[:, 0:E], 0, e)
+        acc = psum.tile([P, 2 * E, 2 * C], F32, name="acc")
+        for m in range(1, 3):
             for e in range(E):
-                multiply(m, e)
-                empty(m, e)
+                multiply(acc[:, (m - 1) * E : m * E], m, e)
+        acc = psum.tile([P, 2 * E, 2 * C], F32, name="acc")
+        for e in range(E):
+            multiply(acc[:, 0:E], 3, e)
 
-        def first(m):
-            nc.vector.tensor_tensor(t1[m][:], y[m][:].indirect(pos1_t[:]), gt[m][:, 0, :], MULT)
+        def fetch(m, r, t0, t1):
+            pos = pos1_t if r == 0 else pos2_t
+            t = keep.tile([P, t1 - t0], F32, name=f"t{r}", bufs=2)
+            nc.vector.tensor_tensor(t[:], y[m][:].indirect(pos[:, t0 // 16 : t1 // 16]), gt[m][:, r, t0:t1], MULT)
+            return t
 
-        def second(m):
-            nc.vector.tensor_tensor(t2[m][:], y[m][:].indirect(pos2_t[:]), gt[m][:, 1, :], MULT)
+        def finish(m, t0, t1, f, s):
+            res = keep.tile([P, t1 - t0], F32, name="res", bufs=4)
+            nc.vector.tensor_tensor(res[:], f, s, ADD)
+            nc.sync.dma_start(out[m * P : (m + 1) * P, t0:t1], res[:])
 
-        def finish(m):
-            nc.vector.tensor_tensor(res[m][:], t1[m][:], t2[m][:], ADD)
-            nc.sync.dma_start(out[m * P : (m + 1) * P, :], res[m][:])
-
-        for m in range(BLOCKS):
-            first(m)
-            if m > 0:
-                finish(m - 1)
-            second(m)
-        finish(BLOCKS - 1)
+        before = None
+        for m in range(BLOCKS - 1):
+            f = fetch(m, 0, 0, T)
+            if before is not None:
+                finish(m - 1, 0, T, *before)
+            before = (f[:], fetch(m, 1, 0, T)[:])
+        last = BLOCKS - 1
+        f = fetch(last, 0, 0, T)
+        finish(last - 1, 0, T, *before)
+        sa = fetch(last, 1, 0, T // 2)
+        sb = fetch(last, 1, T // 2, T)
+        finish(last, 0, T // 2, f[:, 0 : T // 2], sa[:])
+        finish(last, T // 2, T, f[:, T // 2 : T], sb[:])

@@ -1,6 +1,7 @@
 from contextlib import ExitStack
 
 import concourse.mybir as mybir
+from concourse.masks import make_identity
 
 K, T, E, C, N = 1536, 512, 4, 256, 512
 P = 128
@@ -37,14 +38,18 @@ def tile_routed_moe_kernel(tc, xT, w_words, w_scales, b, gate, offs, pos1, pos2,
         xs = keep.tile([P, T], U8, name="xs", align_bytes=64)
         gw = [keep.tile([P, SLOTS], U32, name=f"gw{a}", align_bytes=64) for a in range(PASSES)]
         gs = keep.tile([P, SLOTS], U8, name="gs", align_bytes=64)
-        ww = [keep.tile([P, PASSES, N], U32, name=f"ww{e}", align_bytes=64) for e in range(E)]
+        ww = [
+            [keep.tile([P, 2 * PASSES, N // 2], U32, name=f"ww{h}{g}", align_bytes=64) for g in range(2)] for h in range(2)
+        ]
         ws = keep.tile([P, E, N], U8, name="ws", align_bytes=64)
         bias = keep.tile([P, BLOCKS, E], F32, name="bias")
         gt = [keep.tile([P, 2, T], F32, name=f"gt{m}") for m in range(BLOCKS)]
         y = [keep.tile([P, SLOTS], F32, name=f"y{m}") for m in range(BLOCKS)]
 
+        ident = keep.tile([P, P], F32, name="ident")
+        nc.vector.memset(ws[:].rearrange("p e n -> p (e n)").bitcast(I32), 0)
         nc.gpsimd.memset(xs[:], 0)
-        nc.gpsimd.memset(ws[:].rearrange("p e n -> p (e n)").bitcast(I32), 0)
+        make_identity(nc, ident[:])
 
         def load_x(a):
             src = xT[a * P * PACK : (a + 1) * P * PACK, :]
@@ -57,8 +62,9 @@ def tile_routed_moe_kernel(tc, xT, w_words, w_scales, b, gate, offs, pos1, pos2,
                 ws[rows, :, :].bitcast(I32), w_scales[:, a, 4 * q : 4 * q + 4, :].rearrange("e q n -> q e n").bitcast(I32)
             )
 
-        def load_w(e):
-            nc.sync.dma_start(ww[e][:].bitcast(I32), w_words[e].rearrange("a p n r -> p a (n r)").bitcast(I32))
+        def load_w(h, g):
+            src = w_words[2 * g : 2 * g + 2, :, :, h * (N // 2) : (h + 1) * (N // 2), :]
+            nc.sync.dma_start(ww[h][g][:].bitcast(I32), src.rearrange("e a p n r -> p (e a) (n r)").bitcast(I32))
 
         def load_gate(m):
             nc.sync.dma_start(gt[m][:], gate[:, m * P : (m + 1) * P, :].rearrange("r p t -> p r t"))
@@ -78,14 +84,16 @@ def tile_routed_moe_kernel(tc, xT, w_words, w_scales, b, gate, offs, pos1, pos2,
         load_x(2)
         for i in range(4, 10):
             load_ws(i)
-        load_w(0)
+        load_w(0, 0)
         for i in range(10, 12):
             load_ws(i)
         load_bias()
-        for e in range(1, E):
-            load_w(e)
+        load_w(0, 1)
         load_pos()
-        for m in range(BLOCKS):
+        load_gate(0)
+        load_w(1, 0)
+        load_w(1, 1)
+        for m in range(1, BLOCKS):
             load_gate(m)
 
         def interleave(copy, a, t0, t1):
@@ -103,18 +111,19 @@ def tile_routed_moe_kernel(tc, xT, w_words, w_scales, b, gate, offs, pos1, pos2,
         def gather_scales(s0, s1):
             nc.vector.tensor_copy(gs[:, s0:s1], xs[:].indirect(offs_t[:, s0 // 16 : s1 // 16]))
 
-        def multiply(acc, m, e):
+        def multiply(acc, m, s0, s1):
+            e = s0 // C
             for a in range(PASSES):
                 nc.tensor.matmul_mx(
-                    out=acc[:, e, 0:C],
-                    lhsT=ww[e][:, a, m * P : (m + 1) * P].bitcast(FP8X4),
+                    out=acc,
+                    lhsT=ww[m // 2][e // 2][:, (e % 2) * PASSES + a, (m % 2) * P : (m % 2 + 1) * P].bitcast(FP8X4),
                     lhsT_scale=ws[4 * a : P, e, m * P : (m + 1) * P],
-                    rhs=gw[a][:, e * C : (e + 1) * C].bitcast(FP8X4),
-                    rhs_scale=gs[4 * a : P, e * C : (e + 1) * C],
+                    rhs=gw[a][:, s0:s1].bitcast(FP8X4),
+                    rhs_scale=gs[4 * a : P, s0:s1],
                     start=(a == 0),
                     stop=(a == PASSES - 1),
                 )
-            nc.scalar.activation(y[m][:, e * C : (e + 1) * C], acc[:, e, 0:C], RELU, bias=bias[:, m, e : e + 1])
+            nc.scalar.activation(y[m][:, s0:s1], acc, RELU, bias=bias[:, m, e : e + 1])
 
         interleave(nc.scalar.copy, 0, 0, 192)
         interleave(nc.vector.tensor_copy, 0, 192, T)
@@ -132,21 +141,26 @@ def tile_routed_moe_kernel(tc, xT, w_words, w_scales, b, gate, offs, pos1, pos2,
         quantize(2)
         gather_words(1, 768, 1024)
         acc = psum.tile([P, 2 * E, 2 * C], F32, name="acc")
-        for e in range(E):
+        for e in range(E - 1):
             gather_scales(e * C, (e + 1) * C)
             gather_words(2, e * C, (e + 1) * C)
-            multiply(acc[:, 0:E], 0, e)
+            multiply(acc[:, e, 0:C], 0, e * C, (e + 1) * C)
+        gather_scales(SLOTS - C, SLOTS)
+        for i in range(2):
+            s0 = SLOTS - C + i * (C // 2)
+            gather_words(2, s0, s0 + C // 2)
+            multiply(acc[:, E - 1 + i, 0 : C // 2], 0, s0, s0 + C // 2)
         acc = psum.tile([P, 2 * E, 2 * C], F32, name="acc")
         for m in range(1, 3):
             for e in range(E):
-                multiply(acc[:, (m - 1) * E : m * E], m, e)
+                multiply(acc[:, (m - 1) * E + e, 0:C], m, e * C, (e + 1) * C)
         acc = psum.tile([P, 2 * E, 2 * C], F32, name="acc")
         for e in range(E):
-            multiply(acc[:, 0:E], 3, e)
+            multiply(acc[:, e, 0:C], 3, e * C, (e + 1) * C)
 
         def fetch(m, r, t0, t1):
             pos = pos1_t if r == 0 else pos2_t
-            t = keep.tile([P, t1 - t0], F32, name=f"t{r}", bufs=2)
+            t = keep.tile([P, t1 - t0], F32, name=f"t{r}", bufs=4)
             nc.vector.tensor_tensor(t[:], y[m][:].indirect(pos[:, t0 // 16 : t1 // 16]), gt[m][:, r, t0:t1], MULT)
             return t
 
@@ -155,16 +169,20 @@ def tile_routed_moe_kernel(tc, xT, w_words, w_scales, b, gate, offs, pos1, pos2,
             nc.vector.tensor_tensor(res[:], f, s, ADD)
             nc.sync.dma_start(out[m * P : (m + 1) * P, t0:t1], res[:])
 
-        before = None
-        for m in range(BLOCKS - 1):
-            f = fetch(m, 0, 0, T)
-            if before is not None:
-                finish(m - 1, 0, T, *before)
-            before = (f[:], fetch(m, 1, 0, T)[:])
+        pairs = [(fetch(m, 0, 0, T)[:], fetch(m, 1, 0, T)[:]) for m in range(2)]
         last = BLOCKS - 1
+        f2 = fetch(last - 1, 0, 0, T)
+        s2 = fetch(last - 1, 1, 0, T)
         f = fetch(last, 0, 0, T)
-        finish(last - 1, 0, T, *before)
+        finish(last - 1, 0, T, f2[:], s2[:])
         sa = fetch(last, 1, 0, T // 2)
         sb = fetch(last, 1, T // 2, T)
         finish(last, 0, T // 2, f[:, 0 : T // 2], sa[:])
         finish(last, T // 2, T, f[:, T // 2 : T], sb[:])
+        acc = psum.tile([P, 2 * E, 2 * C], F32, name="acc")
+        for m in range(2):
+            nc.tensor.matmul(acc[:, m, :], ident[:], pairs[m][0], start=True, stop=False)
+            nc.tensor.matmul(acc[:, m, :], ident[:], pairs[m][1], start=False, stop=True)
+            res = keep.tile([P, T], F32, name=f"res{m}")
+            nc.scalar.copy(res[:], acc[:, m, :])
+            nc.scalar.dma_start(out[m * P : (m + 1) * P, :], res[:])

@@ -9,7 +9,15 @@ PACK = 4
 PASSES = K // (P * PACK)
 BLOCKS = N // P
 SLOTS = E * C
+BANKS, BANK = 8, 512
+HALF_N = N // 2
+PAIR = 2
 FLOPS = 2 * K * SLOTS * N
+
+SCALAR_TOKENS = (192, 448, 512)
+
+FIRST_SLOTS = 768
+WINDOW = 2 * T
 
 F32 = mybir.dt.float32
 BF16 = mybir.dt.bfloat16
@@ -29,160 +37,173 @@ def tile_routed_moe_kernel(tc, xT, w_words, w_scales, b, gate, offs, pos1, pos2,
         keep = ctx.enter_context(tc.tile_pool(name="keep", bufs=1))
         psum = ctx.enter_context(tc.psum_pool(name="psum", bufs=1))
 
-        offs_t = keep.tile([P, SLOTS // 16], U16, name="offs_t")
-        pos1_t = keep.tile([P, T // 16], U16, name="pos1_t")
-        pos2_t = keep.tile([P, T // 16], U16, name="pos2_t")
+        slot_tokens = keep.tile([P, SLOTS // 16], U16, name="slot_tokens")
+        first_slots = keep.tile([P, T // 16], U16, name="first_slots")
+        second_slots = keep.tile([P, T // 16], U16, name="second_slots")
+
         raw = [keep.tile([P, PACK, T], F32, name=f"raw{a}") for a in range(PASSES)]
-        xb = [keep.tile([P, T, PACK], BF16, name=f"xb{a}", align_bytes=64) for a in range(PASSES)]
-        xw = [keep.tile([P, T], U32, name=f"xw{a}", align_bytes=64) for a in range(PASSES)]
-        xs = keep.tile([P, T], U8, name="xs", align_bytes=64)
-        gw = [keep.tile([P, SLOTS], U32, name=f"gw{a}", align_bytes=64) for a in range(PASSES)]
-        gs = keep.tile([P, SLOTS], U8, name="gs", align_bytes=64)
-        ww = [
-            [keep.tile([P, 2 * PASSES, N // 2], U32, name=f"ww{h}{g}", align_bytes=64) for g in range(2)] for h in range(2)
+        grouped = [keep.tile([P, T, PACK], BF16, name=f"grouped{a}", align_bytes=64) for a in range(PASSES)]
+        token_words = [
+            keep.tile([P, WINDOW if a < PASSES - 1 else T], I32, name=f"token_words{a}", align_bytes=64)
+            for a in range(PASSES)
         ]
-        ws = keep.tile([P, E, N], U8, name="ws", align_bytes=64)
+        token_scales = keep.tile([P, T], U8, name="token_scales", align_bytes=64)
+        slot_words = [keep.tile([P, SLOTS], U32, name=f"slot_words{a}", align_bytes=64) for a in range(PASSES)]
+        slot_scales = keep.tile([P, SLOTS], U8, name="slot_scales", align_bytes=64)
+
+        weights = [
+            [keep.tile([P, PAIR * PASSES, HALF_N], U32, name=f"weights{h}{i}", align_bytes=64) for i in range(E // PAIR)]
+            for h in range(N // HALF_N)
+        ]
+        weight_scales = keep.tile([P, E, N], U8, name="weight_scales", align_bytes=64)
+
         bias = keep.tile([P, BLOCKS, E], F32, name="bias")
-        gt = [keep.tile([P, 2, T], F32, name=f"gt{m}") for m in range(BLOCKS)]
-        y = [keep.tile([P, SLOTS], F32, name=f"y{m}") for m in range(BLOCKS)]
-
+        gates = [keep.tile([P, 2, T], F32, name=f"gates{m}") for m in range(BLOCKS)]
+        slot_results = [keep.tile([P, SLOTS], F32, name=f"slot_results{m}") for m in range(BLOCKS)]
         ident = keep.tile([P, P], F32, name="ident")
-        nc.vector.memset(ws[:].rearrange("p e n -> p (e n)").bitcast(I32), 0)
-        nc.gpsimd.memset(xs[:], 0)
+
+        nc.gpsimd.memset(token_scales[:], 0)
         make_identity(nc, ident[:])
+        for a in range(PASSES - 1):
+            nc.vector.memset(token_words[a][:, T:WINDOW], 0)
+        nc.gpsimd.memset(weight_scales[:].rearrange("p e n -> p (e n)").bitcast(I32), 0)
 
-        def load_x(a):
-            src = xT[a * P * PACK : (a + 1) * P * PACK, :]
-            nc.sync.dma_start(raw[a][:], src.rearrange("(p j) t -> p j t", j=PACK))
+        def load_tokens(a):
+            rows = xT[a * P * PACK : (a + 1) * P * PACK, :]
+            nc.sync.dma_start(raw[a][:], rows.rearrange("(p j) t -> p j t", j=PACK))
 
-        def load_ws(i):
-            a, q = i // 4, i % 4
+        def load_weight_scales(a, q):
             rows = slice(32 * q + 4 * a, 32 * q + 4 * a + 4)
-            nc.sync.dma_start(
-                ws[rows, :, :].bitcast(I32), w_scales[:, a, 4 * q : 4 * q + 4, :].rearrange("e q n -> q e n").bitcast(I32)
-            )
+            source = w_scales[:, a, 4 * q : 4 * q + 4, :].rearrange("e q n -> q e n")
+            nc.sync.dma_start(weight_scales[rows, :, :].bitcast(I32), source.bitcast(I32))
 
-        def load_w(h, g):
-            src = w_words[2 * g : 2 * g + 2, :, :, h * (N // 2) : (h + 1) * (N // 2), :]
-            nc.sync.dma_start(ww[h][g][:].bitcast(I32), src.rearrange("e a p n r -> p (e a) (n r)").bitcast(I32))
+        def load_weights(h, i):
+            source = w_words[PAIR * i : PAIR * (i + 1), :, :, h * HALF_N : (h + 1) * HALF_N, :]
+            nc.sync.dma_start(weights[h][i][:].bitcast(I32), source.rearrange("e a p n r -> p (e a) (n r)").bitcast(I32))
 
-        def load_gate(m):
-            nc.sync.dma_start(gt[m][:], gate[:, m * P : (m + 1) * P, :].rearrange("r p t -> p r t"))
+        def load_gates(m):
+            nc.sync.dma_start(gates[m][:], gate[:, m * P : (m + 1) * P, :].rearrange("r p t -> p r t"))
 
-        def load_bias():
-            nc.sync.dma_start(bias[:], b.rearrange("(m p) e -> p m e", p=P))
-
-        def load_pos():
-            nc.sync.dma_start(pos1_t[:], pos1)
-            nc.sync.dma_start(pos2_t[:], pos2)
-
-        load_x(0)
-        nc.sync.dma_start(offs_t[:], offs)
-        for i in range(0, 4):
-            load_ws(i)
-        load_x(1)
-        load_x(2)
-        for i in range(4, 10):
-            load_ws(i)
-        load_w(0, 0)
-        for i in range(10, 12):
-            load_ws(i)
-        load_bias()
-        load_w(0, 1)
-        load_pos()
-        load_gate(0)
-        load_w(1, 0)
-        load_w(1, 1)
+        scale_loads = [(a, q) for a in range(PASSES) for q in range(4)]
+        load_tokens(0)
+        nc.sync.dma_start(slot_tokens[:], offs)
+        for a, q in scale_loads[:4]:
+            load_weight_scales(a, q)
+        load_tokens(1)
+        load_tokens(2)
+        for a, q in scale_loads[4:10]:
+            load_weight_scales(a, q)
+        load_weights(0, 0)
+        for a, q in scale_loads[10:]:
+            load_weight_scales(a, q)
+        nc.sync.dma_start(bias[:], b.rearrange("(m p) e -> p m e", p=P))
+        load_weights(0, 1)
+        nc.sync.dma_start(first_slots[:], pos1)
+        nc.sync.dma_start(second_slots[:], pos2)
+        load_gates(0)
+        load_weights(1, 0)
+        load_weights(1, 1)
         for m in range(1, BLOCKS):
-            load_gate(m)
+            load_gates(m)
 
         def interleave(copy, a, t0, t1):
-            dst = xb[a][:, t0:t1, :].rearrange("p (c i) j -> p c j i", i=4)
-            copy(dst, raw[a][:, :, t0:t1].rearrange("p j (c i) -> p c j i", i=4))
+            copy(
+                grouped[a][:, t0:t1, :].rearrange("p (c i) j -> p c j i", i=4),
+                raw[a][:, :, t0:t1].rearrange("p j (c i) -> p c j i", i=4),
+            )
 
         def quantize(a):
             nc.vector.quantize_mx(
-                out=xw[a][:].bitcast(FP8X4), scales=xs[4 * a : P, :], in_=xb[a][:].rearrange("p t j -> p (t j)")
+                out=token_words[a][:, 0:T].bitcast(FP8X4),
+                scales=token_scales[4 * a : P, :],
+                in_=grouped[a][:].rearrange("p t j -> p (t j)"),
             )
 
         def gather_words(a, s0, s1):
-            nc.vector.tensor_copy(gw[a][:, s0:s1], xw[a][:].indirect(offs_t[:, s0 // 16 : s1 // 16]))
+            window = token_words[a][:].bitcast(U32)
+            nc.vector.tensor_copy(slot_words[a][:, s0:s1], window.indirect(slot_tokens[:, s0 // 16 : s1 // 16]))
 
         def gather_scales(s0, s1):
-            nc.vector.tensor_copy(gs[:, s0:s1], xs[:].indirect(offs_t[:, s0 // 16 : s1 // 16]))
+            nc.vector.tensor_copy(
+                slot_scales[:, s0:s1], token_scales[:].indirect(slot_tokens[:, s0 // 16 : s1 // 16])
+            )
 
-        def multiply(acc, m, s0, s1):
+        def multiply(sums, m, s0, s1):
             e = s0 // C
             for a in range(PASSES):
+                words = weights[m * P // HALF_N][e // PAIR][:, (e % PAIR) * PASSES + a, :]
+                n0 = m * P % HALF_N
                 nc.tensor.matmul_mx(
-                    out=acc,
-                    lhsT=ww[m // 2][e // 2][:, (e % 2) * PASSES + a, (m % 2) * P : (m % 2 + 1) * P].bitcast(FP8X4),
-                    lhsT_scale=ws[4 * a : P, e, m * P : (m + 1) * P],
-                    rhs=gw[a][:, s0:s1].bitcast(FP8X4),
-                    rhs_scale=gs[4 * a : P, s0:s1],
+                    out=sums,
+                    lhsT=words[:, n0 : n0 + P].bitcast(FP8X4),
+                    lhsT_scale=weight_scales[4 * a : P, e, m * P : (m + 1) * P],
+                    rhs=slot_words[a][:, s0:s1].bitcast(FP8X4),
+                    rhs_scale=slot_scales[4 * a : P, s0:s1],
                     start=(a == 0),
                     stop=(a == PASSES - 1),
                 )
-            nc.scalar.activation(y[m][:, s0:s1], acc, RELU, bias=bias[:, m, e : e + 1])
+            nc.scalar.activation(slot_results[m][:, s0:s1], sums, RELU, bias=bias[:, m, e : e + 1])
 
-        interleave(nc.scalar.copy, 0, 0, 192)
-        interleave(nc.vector.tensor_copy, 0, 192, T)
+        interleave(nc.scalar.copy, 0, 0, SCALAR_TOKENS[0])
+        interleave(nc.vector.tensor_copy, 0, SCALAR_TOKENS[0], T)
         quantize(0)
-        interleave(nc.scalar.copy, 1, 0, 384)
-        gather_words(0, 0, 384)
-        interleave(nc.vector.tensor_copy, 1, 384, T)
-        gather_words(0, 384, 768)
+        interleave(nc.scalar.copy, 1, 0, SCALAR_TOKENS[1])
+        interleave(nc.vector.tensor_copy, 1, SCALAR_TOKENS[1], T)
+        gather_words(0, 0, FIRST_SLOTS)
         quantize(1)
-        gather_words(0, 768, 1024)
-        interleave(nc.scalar.copy, 2, 0, 256)
-        interleave(nc.scalar.copy, 2, 256, T)
-        gather_words(1, 0, 384)
-        gather_words(1, 384, 768)
+        gather_words(0, FIRST_SLOTS, SLOTS)
+        interleave(nc.scalar.copy, 2, 0, T // 2)
+        interleave(nc.scalar.copy, 2, T // 2, T)
+        gather_words(1, 0, FIRST_SLOTS)
         quantize(2)
-        gather_words(1, 768, 1024)
-        acc = psum.tile([P, 2 * E, 2 * C], F32, name="acc")
+        gather_words(1, FIRST_SLOTS, SLOTS)
+
+        sums = psum.tile([P, BANKS, BANK], F32, name="sums")
         for e in range(E - 1):
             gather_scales(e * C, (e + 1) * C)
             gather_words(2, e * C, (e + 1) * C)
-            multiply(acc[:, e, 0:C], 0, e * C, (e + 1) * C)
+            multiply(sums[:, e, 0:C], 0, e * C, (e + 1) * C)
         gather_scales(SLOTS - C, SLOTS)
         for i in range(2):
             s0 = SLOTS - C + i * (C // 2)
             gather_words(2, s0, s0 + C // 2)
-            multiply(acc[:, E - 1 + i, 0 : C // 2], 0, s0, s0 + C // 2)
-        acc = psum.tile([P, 2 * E, 2 * C], F32, name="acc")
-        for m in range(1, 3):
+            multiply(sums[:, E - 1 + i, 0 : C // 2], 0, s0, s0 + C // 2)
+        sums = psum.tile([P, BANKS, BANK], F32, name="sums")
+        for m in (1, 2):
             for e in range(E):
-                multiply(acc[:, (m - 1) * E + e, 0:C], m, e * C, (e + 1) * C)
-        acc = psum.tile([P, 2 * E, 2 * C], F32, name="acc")
+                multiply(sums[:, (m - 1) * E + e, 0:C], m, e * C, (e + 1) * C)
+        sums = psum.tile([P, BANKS, BANK], F32, name="sums")
         for e in range(E):
-            multiply(acc[:, e, 0:C], 3, e * C, (e + 1) * C)
+            multiply(sums[:, e, 0:C], 3, e * C, (e + 1) * C)
 
         def fetch(m, r, t0, t1):
-            pos = pos1_t if r == 0 else pos2_t
-            t = keep.tile([P, t1 - t0], F32, name=f"t{r}", bufs=4)
-            nc.vector.tensor_tensor(t[:], y[m][:].indirect(pos[:, t0 // 16 : t1 // 16]), gt[m][:, r, t0:t1], MULT)
-            return t
+            slots = (first_slots, second_slots)[r]
+            product = keep.tile([P, t1 - t0], F32, name=f"product{r}", bufs=3)
+            nc.vector.tensor_tensor(
+                product[:], slot_results[m][:].indirect(slots[:, t0 // 16 : t1 // 16]), gates[m][:, r, t0:t1], MULT
+            )
+            return product[:]
 
-        def finish(m, t0, t1, f, s):
-            res = keep.tile([P, t1 - t0], F32, name="res", bufs=4)
-            nc.vector.tensor_tensor(res[:], f, s, ADD)
-            nc.sync.dma_start(out[m * P : (m + 1) * P, t0:t1], res[:])
+        def finish(m, t0, t1, first, second):
+            total = keep.tile([P, t1 - t0], F32, name="total", bufs=4)
+            nc.vector.tensor_tensor(total[:], first, second, ADD)
+            nc.sync.dma_start(out[m * P : (m + 1) * P, t0:t1], total[:])
 
-        pairs = [(fetch(m, 0, 0, T)[:], fetch(m, 1, 0, T)[:]) for m in range(2)]
-        last = BLOCKS - 1
-        f2 = fetch(last - 1, 0, 0, T)
-        s2 = fetch(last - 1, 1, 0, T)
-        f = fetch(last, 0, 0, T)
-        finish(last - 1, 0, T, f2[:], s2[:])
-        sa = fetch(last, 1, 0, T // 2)
-        sb = fetch(last, 1, T // 2, T)
-        finish(last, 0, T // 2, f[:, 0 : T // 2], sa[:])
-        finish(last, T // 2, T, f[:, T // 2 : T], sb[:])
-        acc = psum.tile([P, 2 * E, 2 * C], F32, name="acc")
-        for m in range(2):
-            nc.tensor.matmul(acc[:, m, :], ident[:], pairs[m][0], start=True, stop=False)
-            nc.tensor.matmul(acc[:, m, :], ident[:], pairs[m][1], start=False, stop=True)
-            res = keep.tile([P, T], F32, name=f"res{m}")
-            nc.scalar.copy(res[:], acc[:, m, :])
-            nc.scalar.dma_start(out[m * P : (m + 1) * P, :], res[:])
+        block0 = (fetch(0, 0, 0, T), fetch(0, 1, 0, T))
+        first = fetch(1, 0, 0, T)
+        second = fetch(1, 1, 0, T)
+        following = fetch(2, 0, 0, T)
+        finish(1, 0, T, first, second)
+        first, second = following, fetch(2, 1, 0, T)
+        following = fetch(3, 0, 0, T)
+        finish(2, 0, T, first, second)
+        halves = [(t0, t0 + T // 2, fetch(3, 1, t0, t0 + T // 2)) for t0 in (0, T // 2)]
+        for t0, t1, second in halves:
+            finish(3, t0, t1, following[:, t0:t1], second)
+
+        sums = psum.tile([P, BANKS, BANK], F32, name="sums")
+        for r in range(2):
+            nc.tensor.matmul(sums[:, 0, :], ident[:], block0[r], start=(r == 0), stop=(r == 1))
+        total0 = keep.tile([P, T], F32, name="total0")
+        nc.scalar.copy(total0[:], sums[:, 0, :])
+        nc.scalar.dma_start(out[0:P, :], total0[:])

from contextlib import ExitStack

import concourse.mybir as mybir
from concourse.masks import make_identity

K, T, E, C, N = 1536, 512, 4, 256, 512
P = 128
PACK = 4
PASSES = K // (P * PACK)
BLOCKS = N // P
SLOTS = E * C
BANKS, BANK = 8, 512
HALF_N = N // 2
PAIR = 2
FLOPS = 2 * K * SLOTS * N

SCALAR_TOKENS = (192, 448, 512)

FIRST_SLOTS = 768
WINDOW = 2 * T

F32 = mybir.dt.float32
BF16 = mybir.dt.bfloat16
I32 = mybir.dt.int32
U32 = mybir.dt.uint32
U16 = mybir.dt.uint16
U8 = mybir.dt.uint8
FP8X4 = mybir.dt.float8_e4m3fn_x4
MULT = mybir.AluOpType.mult
ADD = mybir.AluOpType.add
RELU = mybir.ActivationFunctionType.Relu


def tile_routed_moe_kernel(tc, xT, w_words, w_scales, b, gate, offs, pos1, pos2, out):
    nc = tc.nc
    with ExitStack() as ctx:
        keep = ctx.enter_context(tc.tile_pool(name="keep", bufs=1))
        psum = ctx.enter_context(tc.psum_pool(name="psum", bufs=1))

        slot_tokens = keep.tile([P, SLOTS // 16], U16, name="slot_tokens")
        first_slots = keep.tile([P, T // 16], U16, name="first_slots")
        second_slots = keep.tile([P, T // 16], U16, name="second_slots")

        raw = [keep.tile([P, PACK, T], F32, name=f"raw{a}") for a in range(PASSES)]
        grouped = [keep.tile([P, T, PACK], BF16, name=f"grouped{a}", align_bytes=64) for a in range(PASSES)]
        token_words = [
            keep.tile([P, WINDOW if a < PASSES - 1 else T], I32, name=f"token_words{a}", align_bytes=64)
            for a in range(PASSES)
        ]
        token_scales = keep.tile([P, T], U8, name="token_scales", align_bytes=64)
        slot_words = [keep.tile([P, SLOTS], U32, name=f"slot_words{a}", align_bytes=64) for a in range(PASSES)]
        slot_scales = keep.tile([P, SLOTS], U8, name="slot_scales", align_bytes=64)

        weights = [
            [keep.tile([P, PAIR * PASSES, HALF_N], U32, name=f"weights{h}{i}", align_bytes=64) for i in range(E // PAIR)]
            for h in range(N // HALF_N)
        ]
        weight_scales = keep.tile([P, E, N], U8, name="weight_scales", align_bytes=64)

        bias = keep.tile([P, BLOCKS, E], F32, name="bias")
        gates = [keep.tile([P, 2, T], F32, name=f"gates{m}") for m in range(BLOCKS)]
        slot_results = [keep.tile([P, SLOTS], F32, name=f"slot_results{m}") for m in range(BLOCKS)]
        ident = keep.tile([P, P], F32, name="ident")

        nc.gpsimd.memset(token_scales[:], 0)
        make_identity(nc, ident[:])
        for a in range(PASSES - 1):
            nc.vector.memset(token_words[a][:, T:WINDOW], 0)
        nc.gpsimd.memset(weight_scales[:].rearrange("p e n -> p (e n)").bitcast(I32), 0)

        def load_tokens(a):
            rows = xT[a * P * PACK : (a + 1) * P * PACK, :]
            nc.sync.dma_start(raw[a][:], rows.rearrange("(p j) t -> p j t", j=PACK))

        def load_weight_scales(a, q):
            rows = slice(32 * q + 4 * a, 32 * q + 4 * a + 4)
            source = w_scales[:, a, 4 * q : 4 * q + 4, :].rearrange("e q n -> q e n")
            nc.sync.dma_start(weight_scales[rows, :, :].bitcast(I32), source.bitcast(I32))

        def load_weights(h, i):
            source = w_words[PAIR * i : PAIR * (i + 1), :, :, h * HALF_N : (h + 1) * HALF_N, :]
            nc.sync.dma_start(weights[h][i][:].bitcast(I32), source.rearrange("e a p n r -> p (e a) (n r)").bitcast(I32))

        def load_gates(m):
            nc.sync.dma_start(gates[m][:], gate[:, m * P : (m + 1) * P, :].rearrange("r p t -> p r t"))

        scale_loads = [(a, q) for a in range(PASSES) for q in range(4)]
        load_tokens(0)
        nc.sync.dma_start(slot_tokens[:], offs)
        for a, q in scale_loads[:4]:
            load_weight_scales(a, q)
        load_tokens(1)
        load_tokens(2)
        for a, q in scale_loads[4:10]:
            load_weight_scales(a, q)
        load_weights(0, 0)
        for a, q in scale_loads[10:]:
            load_weight_scales(a, q)
        nc.sync.dma_start(bias[:], b.rearrange("(m p) e -> p m e", p=P))
        load_weights(0, 1)
        nc.sync.dma_start(first_slots[:], pos1)
        nc.sync.dma_start(second_slots[:], pos2)
        load_gates(0)
        load_weights(1, 0)
        load_weights(1, 1)
        for m in range(1, BLOCKS):
            load_gates(m)

        def interleave(copy, a, t0, t1):
            copy(
                grouped[a][:, t0:t1, :].rearrange("p (c i) j -> p c j i", i=4),
                raw[a][:, :, t0:t1].rearrange("p j (c i) -> p c j i", i=4),
            )

        def quantize(a):
            nc.vector.quantize_mx(
                out=token_words[a][:, 0:T].bitcast(FP8X4),
                scales=token_scales[4 * a : P, :],
                in_=grouped[a][:].rearrange("p t j -> p (t j)"),
            )

        def gather_words(a, s0, s1):
            window = token_words[a][:].bitcast(U32)
            nc.vector.tensor_copy(slot_words[a][:, s0:s1], window.indirect(slot_tokens[:, s0 // 16 : s1 // 16]))

        def gather_scales(s0, s1):
            nc.vector.tensor_copy(
                slot_scales[:, s0:s1], token_scales[:].indirect(slot_tokens[:, s0 // 16 : s1 // 16])
            )

        def multiply(sums, m, s0, s1):
            e = s0 // C
            for a in range(PASSES):
                words = weights[m * P // HALF_N][e // PAIR][:, (e % PAIR) * PASSES + a, :]
                n0 = m * P % HALF_N
                nc.tensor.matmul_mx(
                    out=sums,
                    lhsT=words[:, n0 : n0 + P].bitcast(FP8X4),
                    lhsT_scale=weight_scales[4 * a : P, e, m * P : (m + 1) * P],
                    rhs=slot_words[a][:, s0:s1].bitcast(FP8X4),
                    rhs_scale=slot_scales[4 * a : P, s0:s1],
                    start=(a == 0),
                    stop=(a == PASSES - 1),
                )
            nc.scalar.activation(slot_results[m][:, s0:s1], sums, RELU, bias=bias[:, m, e : e + 1])

        interleave(nc.scalar.copy, 0, 0, SCALAR_TOKENS[0])
        interleave(nc.vector.tensor_copy, 0, SCALAR_TOKENS[0], T)
        quantize(0)
        interleave(nc.scalar.copy, 1, 0, SCALAR_TOKENS[1])
        interleave(nc.vector.tensor_copy, 1, SCALAR_TOKENS[1], T)
        gather_words(0, 0, FIRST_SLOTS)
        quantize(1)
        gather_words(0, FIRST_SLOTS, SLOTS)
        interleave(nc.scalar.copy, 2, 0, T // 2)
        interleave(nc.scalar.copy, 2, T // 2, T)
        gather_words(1, 0, FIRST_SLOTS)
        quantize(2)
        gather_words(1, FIRST_SLOTS, SLOTS)

        sums = psum.tile([P, BANKS, BANK], F32, name="sums")
        for e in range(E - 1):
            gather_scales(e * C, (e + 1) * C)
            gather_words(2, e * C, (e + 1) * C)
            multiply(sums[:, e, 0:C], 0, e * C, (e + 1) * C)
        gather_scales(SLOTS - C, SLOTS)
        for i in range(2):
            s0 = SLOTS - C + i * (C // 2)
            gather_words(2, s0, s0 + C // 2)
            multiply(sums[:, E - 1 + i, 0 : C // 2], 0, s0, s0 + C // 2)
        sums = psum.tile([P, BANKS, BANK], F32, name="sums")
        for m in (1, 2):
            for e in range(E):
                multiply(sums[:, (m - 1) * E + e, 0:C], m, e * C, (e + 1) * C)
        sums = psum.tile([P, BANKS, BANK], F32, name="sums")
        for e in range(E):
            multiply(sums[:, e, 0:C], 3, e * C, (e + 1) * C)

        def fetch(m, r, t0, t1):
            slots = (first_slots, second_slots)[r]
            product = keep.tile([P, t1 - t0], F32, name=f"product{r}", bufs=3)
            nc.vector.tensor_tensor(
                product[:], slot_results[m][:].indirect(slots[:, t0 // 16 : t1 // 16]), gates[m][:, r, t0:t1], MULT
            )
            return product[:]

        def finish(m, t0, t1, first, second):
            total = keep.tile([P, t1 - t0], F32, name="total", bufs=4)
            nc.vector.tensor_tensor(total[:], first, second, ADD)
            nc.sync.dma_start(out[m * P : (m + 1) * P, t0:t1], total[:])

        block0 = (fetch(0, 0, 0, T), fetch(0, 1, 0, T))
        first = fetch(1, 0, 0, T)
        second = fetch(1, 1, 0, T)
        following = fetch(2, 0, 0, T)
        finish(1, 0, T, first, second)
        first, second = following, fetch(2, 1, 0, T)
        following = fetch(3, 0, 0, T)
        finish(2, 0, T, first, second)
        halves = [(t0, t0 + T // 2, fetch(3, 1, t0, t0 + T // 2)) for t0 in (0, T // 2)]
        for t0, t1, second in halves:
            finish(3, t0, t1, following[:, t0:t1], second)

        sums = psum.tile([P, BANKS, BANK], F32, name="sums")
        for r in range(2):
            nc.tensor.matmul(sums[:, 0, :], ident[:], block0[r], start=(r == 0), stop=(r == 1))
        total0 = keep.tile([P, T], F32, name="total0")
        nc.scalar.copy(total0[:], sums[:, 0, :])
        nc.scalar.dma_start(out[0:P, :], total0[:])
